import numpy as np
import ml_dtypes


def mxq(x, axis, fmt="e4m3"):
    dtype, down = {"e4m3": (ml_dtypes.float8_e4m3fn, 7), "e5m2": (ml_dtypes.float8_e5m2, 14)}[fmt]
    v = np.moveaxis(np.asarray(x, np.float32).astype(ml_dtypes.bfloat16).astype(np.float64), axis, -1)
    blocks = v.reshape(v.shape[:-1] + (-1, 32))
    amax = np.abs(blocks).max(-1, keepdims=True)
    byte = np.maximum(np.where(amax > 0, np.frexp(amax)[1] - 1 + 127, 0) - down, 1)
    scale = np.exp2(byte - 127.0)
    codes = (blocks / scale).astype(np.float32).astype(dtype).astype(np.float64)
    return np.moveaxis((codes * scale).reshape(v.shape), -1, axis)


WIDE = False


def mx_kscale(k):
    if not WIDE:
        return np.ones(k)
    levels = np.array([10, -10, 5, -5, 0])
    if k % 512:
        return np.exp2(np.random.permutation(np.resize(levels, k // 32))).repeat(32)
    a = np.empty((k // 512, 16))
    for p in range(k // 512):
        a[p, :8] = np.random.permutation(np.resize(levels, 8))
        for g in range(8):
            far = levels[np.abs(levels - a[p, g]) >= 10]
            a[p, g + 8] = far[np.random.randint(len(far))]
    return np.exp2(a.ravel()).repeat(32)


def f64(x):
    return np.asarray(x).astype(np.float64)


def striped(idx):
    return np.tile(idx.reshape(-1, 16).T, (8, 1)).astype(np.uint16)


def unstriped(offs):
    return offs[:16].T.reshape(-1).astype(np.int64)


E2M1 = np.array([0.0, 0.5, 1.0, 1.5, 2.0, 3.0, 4.0, 6.0, -0.0, -0.5, -1.0, -1.5, -2.0, -3.0, -4.0, -6.0])


def pack_weight(w, fmt):
    k, n = w.shape
    w = f64(np.asarray(w, np.float32).astype(ml_dtypes.bfloat16)).reshape(k // 32, 32, n)
    amax = np.abs(w).max(1)
    if fmt == "e4m3":
        byte = np.frexp(amax)[1] - 1 + 127 - 7
    else:
        mant, ex = np.frexp(amax / 6.0)
        byte = np.where(mant > 0.5, ex, ex - 1) + 127
    byte = np.clip(np.where(amax > 0, byte, 1), 1, 254)
    scaled = (w * np.exp2(127.0 - byte)[:, None, :]).reshape(k, n).astype(np.float32)
    by_word = np.ascontiguousarray(scaled.reshape(k // 512, 128, 4, n).transpose(0, 1, 3, 2))
    if fmt == "e4m3":
        words = by_word.astype(ml_dtypes.float8_e4m3fn).view(np.uint8)
    else:
        c = by_word.astype(ml_dtypes.float4_e2m1fn).view(np.uint8) & 0xF
        words = (c[..., 0::2] | (c[..., 1::2] << 4)).reshape(k // 512, 128, 2 * n)
    return np.ascontiguousarray(words), np.ascontiguousarray(byte.astype(np.uint8).reshape(k // 512, 16, n))


def unpack_weight(words, scales, fmt):
    g, _, n = scales.shape
    words = np.ascontiguousarray(words).reshape(g, 128, n, -1)
    if fmt == "e4m3":
        vals = words.view(ml_dtypes.float8_e4m3fn).astype(np.float64)
    else:
        nib = np.empty((g, 128, n, 4), np.uint8)
        nib[..., 0::2] = words & 0xF
        nib[..., 1::2] = words >> 4
        vals = E2M1[nib]
    vals = vals * np.repeat(np.exp2(scales.astype(np.float64) - 127.0), 8, axis=1)[..., None]
    return vals.transpose(0, 1, 3, 2).reshape(g * 512, n)


def gelu(v):
    return 0.5 * v * (1.0 + np.tanh(np.sqrt(2.0 / np.pi) * (v + 0.044715 * v**3)))


def striped8(idx):
    return np.concatenate([v.reshape(-1, 16).T for v in idx]).astype(np.uint16)


def unstriped8(offs):
    return np.stack([offs[16 * g:16 * g + 16].T.reshape(-1) for g in range(8)]).astype(np.int64)


def runs(v, idx8):
    k = np.arange(v.shape[0])
    return v[k[:, None], idx8[k % 512 // 64]]


K, K2, H, N, T, S, T2 = 1024, 512, 1024, 512, 2048, 1024, 2048

def setup_inputs():
    n = np.random.standard_normal
    s, s2, u = mx_kscale(K)[:, None], mx_kscale(K2)[:, None], mx_kscale(H)[:, None]
    tab_words, tab_scales = pack_weight(n((K, T)) * s, "e4m3")
    tab2_words, tab2_scales = pack_weight(n((K2, T)) * s2, "e4m3")
    w1 = n((K, H)) / np.sqrt(K) / s * u.T
    w4_words, w4_scales = pack_weight(1.6 * n((K2, H)) / np.sqrt(K2) / s2, "e2m1")
    gain = 1.2 * np.exp(0.3 * n(H)) * u[:, 0]
    w8_words, w8_scales = pack_weight(1.5 * n((H, N)) / np.sqrt(H) / u, "e4m3")
    wb = 1.5 * n((H, N)) / np.sqrt(H) / u
    return {
        "tab_words": tab_words, "tab_scales": tab_scales,
        "offs": striped8(np.stack([np.random.permutation(T)[:S] for _ in range(8)])),
        "tab2_words": tab2_words, "tab2_scales": tab2_scales,
        "offs2": striped(np.random.permutation(T)[:S]),
        "offs3": striped(np.random.permutation(T2)[:S]),
        "w1": w1.astype(np.float32), "w4_words": w4_words, "w4_scales": w4_scales,
        "gain": gain.astype(np.float32),
        "w8_words": w8_words, "w8_scales": w8_scales, "wb": wb.astype(np.float32),
        "wgo": np.exp(0.3 * n((128, S))).astype(np.float32),
        "page1": n((N, T2)).astype(np.float32)}

def reference(tab_words, tab_scales, offs, tab2_words, tab2_scales, offs2, offs3,
              w1, w4_words, w4_scales, gain, w8_words, w8_scales, wb, wgo, page1):
    v = runs(unpack_weight(tab_words, tab_scales, "e4m3"), unstriped8(offs))
    v2 = unpack_weight(tab2_words, tab2_scales, "e4m3")[:, unstriped(offs2)]
    stitch = mxq(f64(w1), 0, "e4m3").T @ v
    fabric = unpack_weight(w4_words, w4_scales, "e2m1").T @ v2
    h = np.maximum(stitch, f64(gain)[:, None] * np.tanh(fabric))
    hq = mxq(h, 0, "e4m3")
    ya = unpack_weight(w8_words, w8_scales, "e4m3").T @ hq
    yb = mxq(f64(wb), 0, "e4m3").T @ hq
    y = ya / (1.0 + np.abs(yb))
    out = f64(page1).copy()
    out[:, unstriped(offs3)] = np.tile(f64(wgo), (N // 128, 1)) * y
    return out

@@ -1,0 +1,257 @@
+from contextlib import ExitStack
+
+import concourse.mybir as mybir
+
+K, K2, H, N, T, S, T2 = 1024, 512, 1024, 512, 2048, 1024, 2048
+FLOPS = 2 * S * (K * H + K2 * H + 2 * H * N)
+
+F32 = mybir.dt.float32
+BF16 = mybir.dt.bfloat16
+I32 = mybir.dt.int32
+U32 = mybir.dt.uint32
+U16 = mybir.dt.uint16
+U8 = mybir.dt.uint8
+FP8X4 = mybir.dt.float8_e4m3fn_x4
+FP4X4 = mybir.dt.float4_e2m1fn_x4
+ACT = mybir.ActivationFunctionType
+ALU = mybir.AluOpType
+
+P = 128
+PACK = 4
+PASS = P * PACK
+CH = 512
+NCH = S // CH
+LIST_COLS = CH // 16
+
+
+def tile_list_stitch_pull_features_kernel(
+    tc, tab_words, tab_scales, offs, tab2_words, tab2_scales, offs2, offs3,
+    w1, w4_words, w4_scales, gain, w8_words, w8_scales, wb, wgo, page1, out,
+):
+    nc = tc.nc
+    with ExitStack() as ctx:
+        keep = ctx.enter_context(tc.tile_pool(name="keep", bufs=1))
+        ring2 = ctx.enter_context(tc.tile_pool(name="ring2", bufs=2))
+        ring3 = ctx.enter_context(tc.tile_pool(name="ring3", bufs=3))
+        ps_s = ctx.enter_context(tc.psum_pool(name="ps_s", bufs=3))
+        ps_v = ctx.enter_context(tc.psum_pool(name="ps_v", bufs=5))
+
+        def words_of(src):
+            return src.rearrange("p t i -> p (t i)").bitcast(I32)
+
+        def load_plane(dst, rows):
+            for d in range(4):
+                nc.sync.dma_start(out=dst[32 * d : 32 * (d + 1), :].bitcast(I32),
+                                  in_=rows[4 * d : 4 * d + 4, :].bitcast(I32).partition_broadcast(8))
+
+        def load_rows(src, tag):
+            raw = keep.tile([P, PACK, PASS], F32, name=tag + "_raw", tag=tag, align_bytes=64)
+            nc.sync.dma_start(out=raw[:], in_=src.rearrange("(p j) c -> p j c", j=PACK))
+            return raw
+
+        def load_table(src, tag):
+            win = keep.tile([P, T], U32, name=tag + "_win", tag=tag, align_bytes=64)
+            nc.sync.dma_start(out=win[:].bitcast(I32), in_=words_of(src))
+            return win
+
+        def load_list(src, name):
+            lst = keep.tile([P, S // 16], U16, name=name)
+            nc.sync.dma_start(lst[:], src)
+            return lst
+
+        def entries(lst, j):
+            return lst[:, LIST_COLS * j : LIST_COLS * (j + 1)]
+
+        def quantize(grouped, name):
+            codes = keep.tile([P, PASS], U32, name=name + "_codes", align_bytes=64)
+            plane = keep.tile([P, PASS], U8, name=name + "_plane", align_bytes=64)
+            nc.vector.quantize_mx(out=codes[:].bitcast(FP8X4), scales=plane[:], in_=grouped)
+            return codes, plane
+
+        def interleave(src, copy, grouped=None):
+            if grouped is None:
+                grouped = ring3.tile([P, PASS * PACK], BF16, name="grouped", align_bytes=64)
+            copy(out=grouped[:].rearrange("p (c i t) -> p c t i", i=4, t=PACK),
+                 in_=src[:].rearrange("p t (c i) -> p c t i", i=4))
+            return grouped[:]
+
+        def interleave_gpsimd(src, name):
+            grouped = keep.tile([P, PASS, PACK], BF16, name=name, align_bytes=64)
+            for c0 in range(0, PASS, P):
+                nc.gpsimd.tensor_scalar(
+                    out=grouped[:, c0 : c0 + P, :], in0=src[:, :, c0 : c0 + P].rearrange("p t c -> p c t"),
+                    scalar1=1.0, scalar2=0.0, op0=ALU.mult, op1=ALU.add)
+            return grouped[:].rearrange("p c t -> p (c t)")
+
+        def deal_and_interleave(raw):
+            grouped = ring3.tile([P, PASS * PACK], BF16, name="grouped", align_bytes=64)
+            nc.scalar.copy(out=grouped[:].rearrange("p (t m j) -> p m j t", t=PACK, j=PACK),
+                           in_=raw[:].rearrange("p j (m t) -> p m j t", t=PACK))
+            return grouped[:]
+
+        v2s_win = keep.tile([P, T], U8, name="v2s_win", align_bytes=64)
+        vs_win = keep.tile([P, T], U8, name="vs_win", align_bytes=64)
+        w4s_raw = keep.tile([P, H], U8, name="w4s_raw", align_bytes=64)
+        w8_plane = keep.tile([P, N], U8, name="w8_plane", align_bytes=64)
+        nc.gpsimd.memset(vs_win[:].bitcast(I32), 0)
+
+        list2 = load_list(offs2, "list2")
+        load_plane(v2s_win, tab2_scales[0])
+        list1 = load_list(offs, "list1")
+        nc.sync.dma_start(out=vs_win[0:P:4, :].bitcast(I32),
+                          in_=tab_scales.rearrange("a q t -> q a t").bitcast(I32))
+        w1_raw = {}
+        w1_raw[0, 0] = load_rows(w1[0:PASS, 0:PASS], "slot0")
+        w4_raw = keep.tile([P, 2 * H], U8, name="w4_raw", align_bytes=64)
+        nc.sync.dma_start(out=w4_raw[:].bitcast(I32), in_=w4_words[0].bitcast(I32))
+        v2_win = load_table(tab2_words[0], "v2_win")
+        load_plane(w4s_raw, w4_scales[0])
+        w1_raw[1, 0] = load_rows(w1[PASS:K, 0:PASS], "slot1")
+        gains = keep.tile([P, H // PASS, PACK], F32, name="gains")
+        nc.sync.dma_start(out=gains[:], in_=gain.rearrange("(b p t) -> p b t", p=P, t=PACK))
+        v_win = [load_table(tab_words[0], "v_win0")]
+        w1_raw[0, 1] = load_rows(w1[0:PASS, PASS:H], "slot2")
+        v_win.append(load_table(tab_words[1], "v_win1"))
+        w1_raw[1, 1] = load_rows(w1[PASS:K, PASS:H], "slot3")
+        wb_raw = [load_rows(wb[PASS * b : PASS * (b + 1), :], "wb%d" % b) for b in range(2)]
+        w8_codes = keep.tile([P, 2, N], U32, name="w8_codes", align_bytes=64)
+        nc.sync.dma_start(out=w8_codes[:].bitcast(I32),
+                          in_=w8_words.rearrange("a p c i -> p a (c i)").bitcast(I32))
+        nc.vector.memset(w8_plane[:].bitcast(I32), 0)
+        for d in range(4):
+            nc.sync.dma_start(out=w8_plane[32 * d : 32 * d + 8, :].bitcast(I32),
+                              in_=w8_scales[:, 4 * d : 4 * d + 4, :].bitcast(I32))
+        factors = keep.tile([P, S], F32, name="factors")
+        nc.sync.dma_start(out=factors[:], in_=wgo)
+        list3 = load_list(offs3, "list3")
+        pages = []
+        for c in range(N // P):
+            page = keep.tile([P, T2], F32, name="page%d" % c)
+            nc.sync.dma_start(out=page[:], in_=page1[P * c : P * (c + 1), :])
+            pages.append(page)
+
+        v2_plane = keep.tile([P, S], U8, name="v2_plane", align_bytes=64)
+        nc.vector.tensor_copy(v2_plane[:], v2s_win[:].indirect(list2[:]))
+        w1_q = {}
+        first_grouped = deal_and_interleave(w1_raw[0, 0])
+        vs_picked = keep.tile([P, S], U8, name="vs_picked", align_bytes=64)
+        nc.vector.tensor_copy(vs_picked[:], vs_win[:].indirect(list1[:]))
+        v_plane = keep.tile([P, S], U8, name="v_plane", tag="slot0", align_bytes=64)
+        nc.vector.tensor_copy(v_plane[:].bitcast(I32), vs_picked[:].bitcast(I32))
+        for r in range(1, 4):
+            nc.scalar.dma_start(out=v_plane[r : r + 101 : 4, :].bitcast(I32),
+                                in_=vs_picked[8 * r : 8 * r + 101 : 4, :].bitcast(I32))
+        w4_dealt = keep.tile([P, 2 * H], U8, name="w4_dealt", align_bytes=64)
+        nc.vector.tensor_copy(
+            out=w4_dealt[:].bitcast(U16).rearrange("p (b t m) -> p b t m", b=2, t=PACK),
+            in_=w4_raw[:].bitcast(U16).rearrange("p (b m t) -> p b t m", b=2, t=PACK))
+
+
+        def gather_words(win, lst, name):
+            picked = []
+            for j in range(NCH):
+                codes = keep.tile([P, CH], U32, name="%s_%d" % (name, j), align_bytes=64)
+                nc.vector.tensor_copy(codes[:], win[:].indirect(entries(lst, j)))
+                picked.append(codes)
+            return picked
+
+        v2_codes = gather_words(v2_win, list2, "v2_codes")
+        w4_plane = keep.tile([P, H], U8, name="w4_plane", align_bytes=64)
+        nc.vector.tensor_copy(
+            out=w4_plane[:].rearrange("p (b t m) -> p b t m", b=2, t=PACK),
+            in_=w4s_raw[:].rearrange("p (b m t) -> p b t m", b=2, t=PACK))
+
+
+        def fabric(b, j, tag):
+            th = keep.tile([P, PACK, CH], F32, name=tag + "_tanh", tag=tag, align_bytes=64)
+            for t in range(PACK):
+                col = PASS * b + P * t
+                acc = ps_s.tile([P, CH], F32, name="acc_s")
+                nc.tensor.matmul_mx(
+                    out=acc[:],
+                    lhsT=w4_dealt[:, 2 * col : 2 * (col + P)].bitcast(FP4X4),
+                    lhsT_scale=w4_plane[:, col : col + P],
+                    rhs=v2_codes[j][:].bitcast(FP8X4),
+                    rhs_scale=v2_plane[:, CH * j : CH * (j + 1)],
+                    start=True, stop=True)
+                nc.scalar.activation(out=th[:, t, :], in_=acc[:], func=ACT.Tanh)
+            return th
+
+        tanhs = {}
+        w1_q[0, 0] = quantize(first_grouped, "w1q00")
+        w1_q[1, 0] = quantize(deal_and_interleave(w1_raw[1, 0]), "w1q10")
+        tanhs[0, 0] = fabric(0, 0, "slot1")
+        v_codes = [gather_words(v_win[0], list1, "v_codes0")]
+        w1_q[0, 1] = quantize(deal_and_interleave(w1_raw[0, 1]), "w1q01")
+        tanhs[0, 1] = fabric(0, 1, "slot2")
+        v_codes.append(gather_words(v_win[1], list1, "v_codes1"))
+        w1_q[1, 1] = quantize(deal_and_interleave(w1_raw[1, 1]), "w1q11")
+        tanhs[1, 0] = fabric(1, 0, "slot3")
+        tanhs[1, 1] = fabric(1, 1, "v2_win")
+
+        def stitch_max(b, j):
+            planes = keep.tile([P, PACK, CH], BF16, name="h_rows%d%d" % (b, j), align_bytes=64)
+            for t in range(PACK):
+                acc = ps_v.tile([P, CH], F32, name="acc_v")
+                for a in range(2):
+                    codes, plane = w1_q[a, b]
+                    nc.tensor.matmul_mx(
+                        out=acc[:],
+                        lhsT=codes[:, P * t : P * (t + 1)].bitcast(FP8X4),
+                        lhsT_scale=plane[:, P * t : P * (t + 1)],
+                        rhs=v_codes[a][j][:].bitcast(FP8X4),
+                        rhs_scale=v_plane[4 * a : P, CH * j : CH * (j + 1)],
+                        start=(a == 0), stop=(a == 1))
+                nc.vector.scalar_tensor_tensor(
+                    out=planes[:, t, :], in0=tanhs[b, j][:, t, :], scalar=gains[:, b, t : t + 1],
+                    in1=acc[:], op0=ALU.mult, op1=ALU.max)
+            return planes
+
+        h_q = {}
+        h_rows = {}
+        h_rows[0, 0] = stitch_max(0, 0)
+        h_rows[0, 1] = stitch_max(0, 1)
+        h_rows[1, 0] = stitch_max(1, 0)
+        h_q[1, 0] = quantize(interleave(h_rows[1, 0], nc.vector.tensor_copy), "hq10")
+        wb_q = [quantize(interleave_gpsimd(wb_raw[b], "wb_grouped%d" % b), "wbq%d" % b) for b in range(2)]
+        h_q[0, 0] = quantize(interleave(h_rows[0, 0], nc.scalar.copy), "hq00")
+        h_rows[1, 1] = stitch_max(1, 1)
+
+        def late_tile(tag):
+            return keep.tile([P, PASS * PACK], BF16, name=tag + "_late", tag=tag, align_bytes=64)
+
+        def second_stage(c, j, damp_tag=None):
+            cols = slice(P * c, P * (c + 1))
+            yb = ps_s.tile([P, CH], F32, name="acc_s")
+            ya = ps_v.tile([P, CH], F32, name="acc_v")
+            for b in range(2):
+                codes, plane = h_q[b, j]
+                nc.tensor.matmul_mx(
+                    out=yb[:], lhsT=wb_q[b][0][:, cols].bitcast(FP8X4), lhsT_scale=wb_q[b][1][:, cols],
+                    rhs=codes[:].bitcast(FP8X4), rhs_scale=plane[:], start=(b == 0), stop=(b == 1))
+            for b in range(2):
+                codes, plane = h_q[b, j]
+                nc.tensor.matmul_mx(
+                    out=ya[:], lhsT=w8_codes[:, b, cols].bitcast(FP8X4), lhsT_scale=w8_plane[4 * b : P, cols],
+                    rhs=codes[:].bitcast(FP8X4), rhs_scale=plane[:], start=(b == 0), stop=(b == 1))
+            if damp_tag is None:
+                damp = ring3.tile([P, CH], F32, name="damp")
+            else:
+                damp = keep.tile([P, CH], F32, name=damp_tag + "_damp", tag=damp_tag, align_bytes=64)
+            nc.scalar.activation(out=damp[:], in_=yb[:], func=ACT.Abs)
+            nc.scalar.activation(out=damp[:], in_=damp[:], func=ACT.Abs_reciprocal_sqrt, bias=1.0)
+            nc.scalar.activation(out=damp[:], in_=damp[:], func=ACT.Square)
+            y = ring2.tile([P, CH], F32, name="y")
+            nc.vector.tensor_tensor(out=y[:], in0=ya[:], in1=damp[:], op=ALU.mult)
+            nc.vector.tensor_tensor(out=pages[c][:].indirect(entries(list3, j)), in0=y[:],
+                                    in1=factors[:, CH * j : CH * (j + 1)], op=ALU.mult)
+
+        second_stage(0, 0, "late0")
+        second_stage(1, 0, "late1")
+        h_q[0, 1] = quantize(interleave(h_rows[0, 1], nc.scalar.copy, late_tile("late0")), "hq01")
+        second_stage(2, 0)
+        h_q[1, 1] = quantize(interleave(h_rows[1, 1], nc.scalar.copy, late_tile("late1")), "hq11")
+        second_stage(3, 0)
+        for c in range(N // P):
+            second_stage(c, 1)
+            nc.sync.dma_start(out=out[P * c : P * (c + 1), :], in_=pages[c][:])

@@ -22,6 +22,7 @@ PASS = P * PACK
 CH = 512
 NCH = S // CH
 LIST_COLS = CH // 16
+HALF = CH // 2
 
 
 def tile_list_stitch_pull_features_kernel(
@@ -75,14 +76,6 @@ def tile_list_stitch_pull_features_kernel(
                  in_=src[:].rearrange("p t (c i) -> p c t i", i=4))
             return grouped[:]
 
-        def interleave_gpsimd(src, name):
-            grouped = keep.tile([P, PASS, PACK], BF16, name=name, align_bytes=64)
-            for c0 in range(0, PASS, P):
-                nc.gpsimd.tensor_scalar(
-                    out=grouped[:, c0 : c0 + P, :], in0=src[:, :, c0 : c0 + P].rearrange("p t c -> p c t"),
-                    scalar1=1.0, scalar2=0.0, op0=ALU.mult, op1=ALU.add)
-            return grouped[:].rearrange("p c t -> p (c t)")
-
         def deal_and_interleave(raw):
             grouped = ring3.tile([P, PASS * PACK], BF16, name="grouped", align_bytes=64)
             nc.scalar.copy(out=grouped[:].rearrange("p (t m j) -> p m j t", t=PACK, j=PACK),
@@ -94,6 +87,7 @@ def tile_list_stitch_pull_features_kernel(
         w4s_raw = keep.tile([P, H], U8, name="w4s_raw", align_bytes=64)
         w8_plane = keep.tile([P, N], U8, name="w8_plane", align_bytes=64)
         nc.gpsimd.memset(vs_win[:].bitcast(I32), 0)
+        nc.gpsimd.memset(w8_plane[:].bitcast(I32), 0)
 
         list2 = load_list(offs2, "list2")
         load_plane(v2s_win, tab2_scales[0])
@@ -108,8 +102,19 @@ def tile_list_stitch_pull_features_kernel(
         load_plane(w4s_raw, w4_scales[0])
         w1_raw[1, 0] = load_rows(w1[PASS:K, 0:PASS], "slot1")
         gains = keep.tile([P, H // PASS, PACK], F32, name="gains")
-        nc.sync.dma_start(out=gains[:], in_=gain.rearrange("(b p t) -> p b t", p=P, t=PACK))
+        nc.gpsimd.dma_start(out=gains[:], in_=gain.rearrange("(b p t) -> p b t", p=P, t=PACK))
         v_win = [load_table(tab_words[0], "v_win0")]
+        v2_plane = keep.tile([P, S], U8, name="v2_plane", align_bytes=64)
+        nc.vector.tensor_copy(v2_plane[:], v2s_win[:].indirect(list2[:]))
+        w1_q = {}
+        first_grouped = deal_and_interleave(w1_raw[0, 0])
+        vs_picked = keep.tile([P, S], U8, name="vs_picked", align_bytes=64)
+        nc.vector.tensor_copy(vs_picked[:], vs_win[:].indirect(list1[:]))
+        v_plane = keep.tile([P, S], U8, name="v_plane", align_bytes=64)
+        nc.vector.tensor_copy(v_plane[:].bitcast(I32), vs_picked[:].bitcast(I32))
+        for r in range(1, 4):
+            nc.sync.dma_start(out=v_plane[r : r + 101 : 4, :].bitcast(I32),
+                                in_=vs_picked[8 * r : 8 * r + 101 : 4, :].bitcast(I32))
         w1_raw[0, 1] = load_rows(w1[0:PASS, PASS:H], "slot2")
         v_win.append(load_table(tab_words[1], "v_win1"))
         w1_raw[1, 1] = load_rows(w1[PASS:K, PASS:H], "slot3")
@@ -117,9 +122,8 @@ def tile_list_stitch_pull_features_kernel(
         w8_codes = keep.tile([P, 2, N], U32, name="w8_codes", align_bytes=64)
         nc.sync.dma_start(out=w8_codes[:].bitcast(I32),
                           in_=w8_words.rearrange("a p c i -> p a (c i)").bitcast(I32))
-        nc.vector.memset(w8_plane[:].bitcast(I32), 0)
         for d in range(4):
-            nc.sync.dma_start(out=w8_plane[32 * d : 32 * d + 8, :].bitcast(I32),
+            nc.gpsimd.dma_start(out=w8_plane[32 * d : 32 * d + 8, :].bitcast(I32),
                               in_=w8_scales[:, 4 * d : 4 * d + 4, :].bitcast(I32))
         factors = keep.tile([P, S], F32, name="factors")
         nc.sync.dma_start(out=factors[:], in_=wgo)
@@ -130,17 +134,6 @@ def tile_list_stitch_pull_features_kernel(
             nc.sync.dma_start(out=page[:], in_=page1[P * c : P * (c + 1), :])
             pages.append(page)
 
-        v2_plane = keep.tile([P, S], U8, name="v2_plane", align_bytes=64)
-        nc.vector.tensor_copy(v2_plane[:], v2s_win[:].indirect(list2[:]))
-        w1_q = {}
-        first_grouped = deal_and_interleave(w1_raw[0, 0])
-        vs_picked = keep.tile([P, S], U8, name="vs_picked", align_bytes=64)
-        nc.vector.tensor_copy(vs_picked[:], vs_win[:].indirect(list1[:]))
-        v_plane = keep.tile([P, S], U8, name="v_plane", tag="slot0", align_bytes=64)
-        nc.vector.tensor_copy(v_plane[:].bitcast(I32), vs_picked[:].bitcast(I32))
-        for r in range(1, 4):
-            nc.scalar.dma_start(out=v_plane[r : r + 101 : 4, :].bitcast(I32),
-                                in_=vs_picked[8 * r : 8 * r + 101 : 4, :].bitcast(I32))
         w4_dealt = keep.tile([P, 2 * H], U8, name="w4_dealt", align_bytes=64)
         nc.vector.tensor_copy(
             out=w4_dealt[:].bitcast(U16).rearrange("p (b t m) -> p b t m", b=2, t=PACK),
@@ -183,39 +176,43 @@ def tile_list_stitch_pull_features_kernel(
         tanhs[0, 0] = fabric(0, 0, "slot1")
         v_codes = [gather_words(v_win[0], list1, "v_codes0")]
         w1_q[0, 1] = quantize(deal_and_interleave(w1_raw[0, 1]), "w1q01")
-        tanhs[0, 1] = fabric(0, 1, "slot2")
+        tanhs[1, 0] = fabric(1, 0, "slot2")
         v_codes.append(gather_words(v_win[1], list1, "v_codes1"))
         w1_q[1, 1] = quantize(deal_and_interleave(w1_raw[1, 1]), "w1q11")
-        tanhs[1, 0] = fabric(1, 0, "slot3")
-        tanhs[1, 1] = fabric(1, 1, "v2_win")
 
-        def stitch_max(b, j):
+        def stitch_max(b, j, early_first_pass):
             planes = keep.tile([P, PACK, CH], BF16, name="h_rows%d%d" % (b, j), align_bytes=64)
-            for t in range(PACK):
-                acc = ps_v.tile([P, CH], F32, name="acc_v")
-                for a in range(2):
+            accs = [ps_v.tile([P, CH], F32, name="acc_v") for t in range(PACK)]
+            passes = [(a, t) for a in range(2) for t in range(PACK)]
+            if not early_first_pass:
+                passes = [(a, t) for t in range(PACK) for a in range(2)]
+            for a, t in passes:
                     codes, plane = w1_q[a, b]
                     nc.tensor.matmul_mx(
-                        out=acc[:],
+                        out=accs[t][:],
                         lhsT=codes[:, P * t : P * (t + 1)].bitcast(FP8X4),
                         lhsT_scale=plane[:, P * t : P * (t + 1)],
                         rhs=v_codes[a][j][:].bitcast(FP8X4),
                         rhs_scale=v_plane[4 * a : P, CH * j : CH * (j + 1)],
                         start=(a == 0), stop=(a == 1))
+            for t in range(PACK):
                 nc.vector.scalar_tensor_tensor(
                     out=planes[:, t, :], in0=tanhs[b, j][:, t, :], scalar=gains[:, b, t : t + 1],
-                    in1=acc[:], op0=ALU.mult, op1=ALU.max)
+                    in1=accs[t][:], op0=ALU.mult, op1=ALU.max)
             return planes
 
         h_q = {}
         h_rows = {}
-        h_rows[0, 0] = stitch_max(0, 0)
-        h_rows[0, 1] = stitch_max(0, 1)
-        h_rows[1, 0] = stitch_max(1, 0)
-        h_q[1, 0] = quantize(interleave(h_rows[1, 0], nc.vector.tensor_copy), "hq10")
-        wb_q = [quantize(interleave_gpsimd(wb_raw[b], "wb_grouped%d" % b), "wbq%d" % b) for b in range(2)]
-        h_q[0, 0] = quantize(interleave(h_rows[0, 0], nc.scalar.copy), "hq00")
-        h_rows[1, 1] = stitch_max(1, 1)
+        h_rows[0, 0] = stitch_max(0, 0, True)
+        h_rows[1, 0] = stitch_max(1, 0, True)
+        grouped00 = interleave(h_rows[0, 0], nc.scalar.copy)
+        wb_q = [quantize(interleave(wb_raw[0], nc.vector.tensor_copy), "wbq0"),
+                quantize(interleave(wb_raw[1], nc.vector.tensor_copy), "wbq1")]
+        h_q[0, 0] = quantize(grouped00, "hq00")
+        h_q[1, 0] = quantize(interleave(h_rows[1, 0], nc.scalar.copy), "hq10")
+        tanhs[0, 1] = fabric(0, 1, "slot3")
+        tanhs[1, 1] = fabric(1, 1, "slot0")
+        h_rows[0, 1] = stitch_max(0, 1, False)
 
         def late_tile(tag):
             return keep.tile([P, PASS * PACK], BF16, name=tag + "_late", tag=tag, align_bytes=64)
@@ -241,12 +238,19 @@ def tile_list_stitch_pull_features_kernel(
             nc.scalar.activation(out=damp[:], in_=yb[:], func=ACT.Abs)
             nc.scalar.activation(out=damp[:], in_=damp[:], func=ACT.Abs_reciprocal_sqrt, bias=1.0)
             nc.scalar.activation(out=damp[:], in_=damp[:], func=ACT.Square)
-            y = ring2.tile([P, CH], F32, name="y")
-            nc.vector.tensor_tensor(out=y[:], in0=ya[:], in1=damp[:], op=ALU.mult)
-            nc.vector.tensor_tensor(out=pages[c][:].indirect(entries(list3, j)), in0=y[:],
-                                    in1=factors[:, CH * j : CH * (j + 1)], op=ALU.mult)
+            ys = []
+            for u in range(2):
+                y = ring2.tile([P, HALF], F32, name="y%d" % u)
+                nc.vector.tensor_tensor(out=y[:], in0=ya[:, HALF * u : HALF * (u + 1)],
+                                        in1=damp[:, HALF * u : HALF * (u + 1)], op=ALU.mult)
+                ys.append(y)
+            for u in range(2):
+                first = CH * j + HALF * u
+                nc.vector.tensor_tensor(out=pages[c][:].indirect(list3[:, first // 16 : (first + HALF) // 16]),
+                                        in0=ys[u][:], in1=factors[:, first : first + HALF], op=ALU.mult)
 
         second_stage(0, 0, "late0")
+        h_rows[1, 1] = stitch_max(1, 1, False)
         second_stage(1, 0, "late1")
         h_q[0, 1] = quantize(interleave(h_rows[0, 1], nc.scalar.copy, late_tile("late0")), "hq01")
         second_stage(2, 0)

@@ -217,7 +217,7 @@ def tile_list_stitch_pull_features_kernel(
         def late_tile(tag):
             return keep.tile([P, PASS * PACK], BF16, name=tag + "_late", tag=tag, align_bytes=64)
 
-        def second_stage(c, j, damp_tag=None):
+        def second_stage(c, j, damp_tag=None, on_gpsimd=True):
             cols = slice(P * c, P * (c + 1))
             yb = ps_s.tile([P, CH], F32, name="acc_s")
             ya = ps_v.tile([P, CH], F32, name="acc_v")
@@ -238,6 +238,15 @@ def tile_list_stitch_pull_features_kernel(
             nc.scalar.activation(out=damp[:], in_=yb[:], func=ACT.Abs)
             nc.scalar.activation(out=damp[:], in_=damp[:], func=ACT.Abs_reciprocal_sqrt, bias=1.0)
             nc.scalar.activation(out=damp[:], in_=damp[:], func=ACT.Square)
+            if on_gpsimd:
+                sums = ring3.tile([P, CH], F32, name="sums")
+                nc.scalar.copy(out=sums[:], in_=ya[:])
+                weight = ring2.tile([P, CH], F32, name="weight")
+                nc.gpsimd.tensor_tensor(out=weight[:], in0=damp[:], in1=factors[:, CH * j : CH * (j + 1)], op=ALU.mult)
+                placed = ring3.tile([P, CH], F32, name="placed")
+                nc.gpsimd.tensor_tensor(out=placed[:], in0=sums[:], in1=weight[:], op=ALU.mult)
+                nc.vector.tensor_copy(pages[c][:].indirect(entries(list3, j)), placed[:])
+                return
             ys = []
             for u in range(2):
                 y = ring2.tile([P, HALF], F32, name="y%d" % u)
@@ -249,9 +258,9 @@ def tile_list_stitch_pull_features_kernel(
                 nc.vector.tensor_tensor(out=pages[c][:].indirect(list3[:, first // 16 : (first + HALF) // 16]),
                                         in0=ys[u][:], in1=factors[:, first : first + HALF], op=ALU.mult)
 
-        second_stage(0, 0, "late0")
+        second_stage(0, 0, "late0", False)
         h_rows[1, 1] = stitch_max(1, 1, False)
-        second_stage(1, 0, "late1")
+        second_stage(1, 0, "late1", False)
         h_q[0, 1] = quantize(interleave(h_rows[0, 1], nc.scalar.copy, late_tile("late0")), "hq01")
         second_stage(2, 0)
         h_q[1, 1] = quantize(interleave(h_rows[1, 1], nc.scalar.copy, late_tile("late1")), "hq11")

@@ -262,9 +262,9 @@ def tile_list_stitch_pull_features_kernel(
         h_rows[1, 1] = stitch_max(1, 1, False)
         second_stage(1, 0, "late1", False)
         h_q[0, 1] = quantize(interleave(h_rows[0, 1], nc.scalar.copy, late_tile("late0")), "hq01")
-        second_stage(2, 0)
         h_q[1, 1] = quantize(interleave(h_rows[1, 1], nc.scalar.copy, late_tile("late1")), "hq11")
-        second_stage(3, 0)
+        second_stage(2, 0, None, False)
+        second_stage(3, 0, None, False)
         for c in range(N // P):
             second_stage(c, 1)
             nc.sync.dma_start(out=out[P * c : P * (c + 1), :], in_=pages[c][:])

@@ -19,10 +19,15 @@ ALU = mybir.AluOpType
 P = 128
 PACK = 4
 PASS = P * PACK
-CH = 512
-NCH = S // CH
-LIST_COLS = CH // 16
-HALF = CH // 2
+QUADRANT = 32
+QUADRANTS = P // QUADRANT
+GROUP = 16
+CHUNK = 512
+CHUNKS = S // CHUNK
+HALF = CHUNK // 2
+LINE = 4
+SCALAR_BANKS = 3
+VECTOR_BANKS = 5
 
 
 def tile_list_stitch_pull_features_kernel(
@@ -34,16 +39,22 @@ def tile_list_stitch_pull_features_kernel(
         keep = ctx.enter_context(tc.tile_pool(name="keep", bufs=1))
         ring2 = ctx.enter_context(tc.tile_pool(name="ring2", bufs=2))
         ring3 = ctx.enter_context(tc.tile_pool(name="ring3", bufs=3))
-        ps_s = ctx.enter_context(tc.psum_pool(name="ps_s", bufs=3))
-        ps_v = ctx.enter_context(tc.psum_pool(name="ps_v", bufs=5))
+        ps_s = ctx.enter_context(tc.psum_pool(name="ps_s", bufs=SCALAR_BANKS))
+        ps_v = ctx.enter_context(tc.psum_pool(name="ps_v", bufs=VECTOR_BANKS))
 
-        def words_of(src):
-            return src.rearrange("p t i -> p (t i)").bitcast(I32)
+        def load_list(src, name):
+            offsets = keep.tile([P, S // GROUP], U16, name=name)
+            nc.sync.dma_start(offsets[:], src)
+            return offsets
+
+        def entries(offsets, first, count):
+            return offsets[:, first // GROUP : (first + count) // GROUP]
 
         def load_plane(dst, rows):
-            for d in range(4):
-                nc.sync.dma_start(out=dst[32 * d : 32 * (d + 1), :].bitcast(I32),
-                                  in_=rows[4 * d : 4 * d + 4, :].bitcast(I32).partition_broadcast(8))
+            for d in range(QUADRANTS):
+                nc.sync.dma_start(
+                    out=dst[QUADRANT * d : QUADRANT * (d + 1), :].bitcast(I32),
+                    in_=rows[PACK * d : PACK * (d + 1), :].bitcast(I32).partition_broadcast(QUADRANT // PACK))
 
         def load_rows(src, tag):
             raw = keep.tile([P, PACK, PASS], F32, name=tag + "_raw", tag=tag, align_bytes=64)
@@ -51,36 +62,37 @@ def tile_list_stitch_pull_features_kernel(
             return raw
 
         def load_table(src, tag):
-            win = keep.tile([P, T], U32, name=tag + "_win", tag=tag, align_bytes=64)
-            nc.sync.dma_start(out=win[:].bitcast(I32), in_=words_of(src))
-            return win
+            window = keep.tile([P, T], U32, name=tag + "_win", tag=tag, align_bytes=64)
+            nc.sync.dma_start(out=window[:].bitcast(I32), in_=src.rearrange("p t i -> p (t i)").bitcast(I32))
+            return window
 
-        def load_list(src, name):
-            lst = keep.tile([P, S // 16], U16, name=name)
-            nc.sync.dma_start(lst[:], src)
-            return lst
+        def gather_words(window, offsets, name):
+            picked = []
+            for j in range(CHUNKS):
+                codes = keep.tile([P, CHUNK], U32, name="%s_%d" % (name, j), align_bytes=64)
+                nc.vector.tensor_copy(codes[:], window[:].indirect(entries(offsets, CHUNK * j, CHUNK)))
+                picked.append(codes)
+            return picked
 
-        def entries(lst, j):
-            return lst[:, LIST_COLS * j : LIST_COLS * (j + 1)]
+        def next_grouped():
+            return ring3.tile([P, PASS * PACK], BF16, name="grouped", align_bytes=64)
+
+        def interleave(rows, copy, grouped):
+            copy(out=grouped[:].rearrange("p (c i t) -> p c t i", i=LINE, t=PACK),
+                 in_=rows[:].rearrange("p t (c i) -> p c t i", i=LINE))
+            return grouped[:]
+
+        def deal_and_interleave(raw):
+            grouped = next_grouped()
+            nc.scalar.copy(out=grouped[:].rearrange("p (t m j) -> p m j t", t=PACK, j=PACK),
+                           in_=raw[:].rearrange("p j (m t) -> p m j t", t=PACK))
+            return grouped[:]
 
         def quantize(grouped, name):
             codes = keep.tile([P, PASS], U32, name=name + "_codes", align_bytes=64)
             plane = keep.tile([P, PASS], U8, name=name + "_plane", align_bytes=64)
             nc.vector.quantize_mx(out=codes[:].bitcast(FP8X4), scales=plane[:], in_=grouped)
             return codes, plane
-
-        def interleave(src, copy, grouped=None):
-            if grouped is None:
-                grouped = ring3.tile([P, PASS * PACK], BF16, name="grouped", align_bytes=64)
-            copy(out=grouped[:].rearrange("p (c i t) -> p c t i", i=4, t=PACK),
-                 in_=src[:].rearrange("p t (c i) -> p c t i", i=4))
-            return grouped[:]
-
-        def deal_and_interleave(raw):
-            grouped = ring3.tile([P, PASS * PACK], BF16, name="grouped", align_bytes=64)
-            nc.scalar.copy(out=grouped[:].rearrange("p (t m j) -> p m j t", t=PACK, j=PACK),
-                           in_=raw[:].rearrange("p j (m t) -> p m j t", t=PACK))
-            return grouped[:]
 
         v2s_win = keep.tile([P, T], U8, name="v2s_win", align_bytes=64)
         vs_win = keep.tile([P, T], U8, name="vs_win", align_bytes=64)
@@ -92,7 +104,7 @@ def tile_list_stitch_pull_features_kernel(
         list2 = load_list(offs2, "list2")
         load_plane(v2s_win, tab2_scales[0])
         list1 = load_list(offs, "list1")
-        nc.sync.dma_start(out=vs_win[0:P:4, :].bitcast(I32),
+        nc.sync.dma_start(out=vs_win[0:P:PACK, :].bitcast(I32),
                           in_=tab_scales.rearrange("a q t -> q a t").bitcast(I32))
         w1_raw = {}
         w1_raw[0, 0] = load_rows(w1[0:PASS, 0:PASS], "slot0")
@@ -104,27 +116,29 @@ def tile_list_stitch_pull_features_kernel(
         gains = keep.tile([P, H // PASS, PACK], F32, name="gains")
         nc.gpsimd.dma_start(out=gains[:], in_=gain.rearrange("(b p t) -> p b t", p=P, t=PACK))
         v_win = [load_table(tab_words[0], "v_win0")]
+
         v2_plane = keep.tile([P, S], U8, name="v2_plane", align_bytes=64)
         nc.vector.tensor_copy(v2_plane[:], v2s_win[:].indirect(list2[:]))
-        w1_q = {}
         first_grouped = deal_and_interleave(w1_raw[0, 0])
         vs_picked = keep.tile([P, S], U8, name="vs_picked", align_bytes=64)
         nc.vector.tensor_copy(vs_picked[:], vs_win[:].indirect(list1[:]))
         v_plane = keep.tile([P, S], U8, name="v_plane", align_bytes=64)
         nc.vector.tensor_copy(v_plane[:].bitcast(I32), vs_picked[:].bitcast(I32))
-        for r in range(1, 4):
-            nc.sync.dma_start(out=v_plane[r : r + 101 : 4, :].bitcast(I32),
-                                in_=vs_picked[8 * r : 8 * r + 101 : 4, :].bitcast(I32))
+        span = QUADRANT * (QUADRANTS - 1) + PACK + 1
+        for r in range(1, PACK):
+            nc.sync.dma_start(out=v_plane[r : r + span : PACK, :].bitcast(I32),
+                              in_=vs_picked[8 * r : 8 * r + span : PACK, :].bitcast(I32))
+
         w1_raw[0, 1] = load_rows(w1[0:PASS, PASS:H], "slot2")
         v_win.append(load_table(tab_words[1], "v_win1"))
         w1_raw[1, 1] = load_rows(w1[PASS:K, PASS:H], "slot3")
-        wb_raw = [load_rows(wb[PASS * b : PASS * (b + 1), :], "wb%d" % b) for b in range(2)]
-        w8_codes = keep.tile([P, 2, N], U32, name="w8_codes", align_bytes=64)
+        wb_raw = [load_rows(wb[PASS * b : PASS * (b + 1), :], "wb%d" % b) for b in range(H // PASS)]
+        w8_codes = keep.tile([P, H // PASS, N], U32, name="w8_codes", align_bytes=64)
         nc.sync.dma_start(out=w8_codes[:].bitcast(I32),
                           in_=w8_words.rearrange("a p c i -> p a (c i)").bitcast(I32))
-        for d in range(4):
-            nc.gpsimd.dma_start(out=w8_plane[32 * d : 32 * d + 8, :].bitcast(I32),
-                              in_=w8_scales[:, 4 * d : 4 * d + 4, :].bitcast(I32))
+        for d in range(QUADRANTS):
+            nc.gpsimd.dma_start(out=w8_plane[QUADRANT * d : QUADRANT * d + 2 * PACK, :].bitcast(I32),
+                                in_=w8_scales[:, PACK * d : PACK * (d + 1), :].bitcast(I32))
         factors = keep.tile([P, S], F32, name="factors")
         nc.sync.dma_start(out=factors[:], in_=wgo)
         list3 = load_list(offs3, "list3")
@@ -136,135 +150,140 @@ def tile_list_stitch_pull_features_kernel(
 
         w4_dealt = keep.tile([P, 2 * H], U8, name="w4_dealt", align_bytes=64)
         nc.vector.tensor_copy(
-            out=w4_dealt[:].bitcast(U16).rearrange("p (b t m) -> p b t m", b=2, t=PACK),
-            in_=w4_raw[:].bitcast(U16).rearrange("p (b m t) -> p b t m", b=2, t=PACK))
-
-
-        def gather_words(win, lst, name):
-            picked = []
-            for j in range(NCH):
-                codes = keep.tile([P, CH], U32, name="%s_%d" % (name, j), align_bytes=64)
-                nc.vector.tensor_copy(codes[:], win[:].indirect(entries(lst, j)))
-                picked.append(codes)
-            return picked
-
+            out=w4_dealt[:].bitcast(U16).rearrange("p (b t m) -> p b t m", b=H // PASS, t=PACK),
+            in_=w4_raw[:].bitcast(U16).rearrange("p (b m t) -> p b t m", b=H // PASS, t=PACK))
         v2_codes = gather_words(v2_win, list2, "v2_codes")
         w4_plane = keep.tile([P, H], U8, name="w4_plane", align_bytes=64)
         nc.vector.tensor_copy(
-            out=w4_plane[:].rearrange("p (b t m) -> p b t m", b=2, t=PACK),
-            in_=w4s_raw[:].rearrange("p (b m t) -> p b t m", b=2, t=PACK))
+            out=w4_plane[:].rearrange("p (b t m) -> p b t m", b=H // PASS, t=PACK),
+            in_=w4s_raw[:].rearrange("p (b m t) -> p b t m", b=H // PASS, t=PACK))
 
-
-        def fabric(b, j, tag):
-            th = keep.tile([P, PACK, CH], F32, name=tag + "_tanh", tag=tag, align_bytes=64)
+        def fabric_tanh(b, j, tag):
+            tanh = keep.tile([P, PACK, CHUNK], F32, name=tag + "_tanh", tag=tag, align_bytes=64)
             for t in range(PACK):
                 col = PASS * b + P * t
-                acc = ps_s.tile([P, CH], F32, name="acc_s")
+                acc = ps_s.tile([P, CHUNK], F32, name="acc_s")
                 nc.tensor.matmul_mx(
                     out=acc[:],
                     lhsT=w4_dealt[:, 2 * col : 2 * (col + P)].bitcast(FP4X4),
                     lhsT_scale=w4_plane[:, col : col + P],
                     rhs=v2_codes[j][:].bitcast(FP8X4),
-                    rhs_scale=v2_plane[:, CH * j : CH * (j + 1)],
+                    rhs_scale=v2_plane[:, CHUNK * j : CHUNK * (j + 1)],
                     start=True, stop=True)
-                nc.scalar.activation(out=th[:, t, :], in_=acc[:], func=ACT.Tanh)
-            return th
+                nc.scalar.activation(out=tanh[:, t, :], in_=acc[:], func=ACT.Tanh)
+            return tanh
 
+        w1_q = {}
         tanhs = {}
         w1_q[0, 0] = quantize(first_grouped, "w1q00")
         w1_q[1, 0] = quantize(deal_and_interleave(w1_raw[1, 0]), "w1q10")
-        tanhs[0, 0] = fabric(0, 0, "slot1")
+        tanhs[0, 0] = fabric_tanh(0, 0, "slot1")
         v_codes = [gather_words(v_win[0], list1, "v_codes0")]
         w1_q[0, 1] = quantize(deal_and_interleave(w1_raw[0, 1]), "w1q01")
-        tanhs[1, 0] = fabric(1, 0, "slot2")
+        tanhs[1, 0] = fabric_tanh(1, 0, "slot2")
         v_codes.append(gather_words(v_win[1], list1, "v_codes1"))
         w1_q[1, 1] = quantize(deal_and_interleave(w1_raw[1, 1]), "w1q11")
 
-        def stitch_max(b, j, early_first_pass):
-            planes = keep.tile([P, PACK, CH], BF16, name="h_rows%d%d" % (b, j), align_bytes=64)
-            accs = [ps_v.tile([P, CH], F32, name="acc_v") for t in range(PACK)]
-            passes = [(a, t) for a in range(2) for t in range(PACK)]
-            if not early_first_pass:
-                passes = [(a, t) for t in range(PACK) for a in range(2)]
-            for a, t in passes:
-                    codes, plane = w1_q[a, b]
-                    nc.tensor.matmul_mx(
-                        out=accs[t][:],
-                        lhsT=codes[:, P * t : P * (t + 1)].bitcast(FP8X4),
-                        lhsT_scale=plane[:, P * t : P * (t + 1)],
-                        rhs=v_codes[a][j][:].bitcast(FP8X4),
-                        rhs_scale=v_plane[4 * a : P, CH * j : CH * (j + 1)],
-                        start=(a == 0), stop=(a == 1))
+        pass_by_pass = [(a, t) for a in range(K // PASS) for t in range(PACK)]
+        bank_by_bank = [(a, t) for t in range(PACK) for a in range(K // PASS)]
+
+        def stitch_max(b, j, order):
+            rows = keep.tile([P, PACK, CHUNK], BF16, name="h_rows%d%d" % (b, j), align_bytes=64)
+            accs = [ps_v.tile([P, CHUNK], F32, name="acc_v") for t in range(PACK)]
+            for a, t in order:
+                codes, plane = w1_q[a, b]
+                nc.tensor.matmul_mx(
+                    out=accs[t][:],
+                    lhsT=codes[:, P * t : P * (t + 1)].bitcast(FP8X4),
+                    lhsT_scale=plane[:, P * t : P * (t + 1)],
+                    rhs=v_codes[a][j][:].bitcast(FP8X4),
+                    rhs_scale=v_plane[PACK * a : P, CHUNK * j : CHUNK * (j + 1)],
+                    start=(a == 0), stop=(a == K // PASS - 1))
             for t in range(PACK):
                 nc.vector.scalar_tensor_tensor(
-                    out=planes[:, t, :], in0=tanhs[b, j][:, t, :], scalar=gains[:, b, t : t + 1],
+                    out=rows[:, t, :], in0=tanhs[b, j][:, t, :], scalar=gains[:, b, t : t + 1],
                     in1=accs[t][:], op0=ALU.mult, op1=ALU.max)
-            return planes
+            return rows
 
         h_q = {}
         h_rows = {}
-        h_rows[0, 0] = stitch_max(0, 0, True)
-        h_rows[1, 0] = stitch_max(1, 0, True)
-        grouped00 = interleave(h_rows[0, 0], nc.scalar.copy)
-        wb_q = [quantize(interleave(wb_raw[0], nc.vector.tensor_copy), "wbq0"),
-                quantize(interleave(wb_raw[1], nc.vector.tensor_copy), "wbq1")]
-        h_q[0, 0] = quantize(grouped00, "hq00")
-        h_q[1, 0] = quantize(interleave(h_rows[1, 0], nc.scalar.copy), "hq10")
-        tanhs[0, 1] = fabric(0, 1, "slot3")
-        tanhs[1, 1] = fabric(1, 1, "slot0")
-        h_rows[0, 1] = stitch_max(0, 1, False)
+        h_rows[0, 0] = stitch_max(0, 0, pass_by_pass)
+        h_rows[1, 0] = stitch_max(1, 0, pass_by_pass)
+        h_grouped = interleave(h_rows[0, 0], nc.scalar.copy, next_grouped())
+        wb_q = [quantize(interleave(wb_raw[b], nc.vector.tensor_copy, next_grouped()), "wbq%d" % b)
+                for b in range(H // PASS)]
+        h_q[0, 0] = quantize(h_grouped, "hq00")
+        h_q[1, 0] = quantize(interleave(h_rows[1, 0], nc.scalar.copy, next_grouped()), "hq10")
+        tanhs[0, 1] = fabric_tanh(0, 1, "slot3")
+        tanhs[1, 1] = fabric_tanh(1, 1, "slot0")
+        preload = keep.tile([P, 1], F32, name="preload")
+        nc.scalar.activation(out=preload[:], in_=tanhs[1, 1][:, PACK - 1, CHUNK - 1 : CHUNK],
+                             func=ACT.Abs_reciprocal_sqrt, bias=2.0)
+        h_rows[0, 1] = stitch_max(0, 1, bank_by_bank)
 
-        def late_tile(tag):
-            return keep.tile([P, PASS * PACK], BF16, name=tag + "_late", tag=tag, align_bytes=64)
-
-        def second_stage(c, j, damp_tag=None, on_gpsimd=True):
+        def products(c, j):
             cols = slice(P * c, P * (c + 1))
-            yb = ps_s.tile([P, CH], F32, name="acc_s")
-            ya = ps_v.tile([P, CH], F32, name="acc_v")
-            for b in range(2):
+            yb = ps_s.tile([P, CHUNK], F32, name="acc_s")
+            ya = ps_v.tile([P, CHUNK], F32, name="acc_v")
+            for b in range(H // PASS):
                 codes, plane = h_q[b, j]
                 nc.tensor.matmul_mx(
                     out=yb[:], lhsT=wb_q[b][0][:, cols].bitcast(FP8X4), lhsT_scale=wb_q[b][1][:, cols],
-                    rhs=codes[:].bitcast(FP8X4), rhs_scale=plane[:], start=(b == 0), stop=(b == 1))
-            for b in range(2):
+                    rhs=codes[:].bitcast(FP8X4), rhs_scale=plane[:],
+                    start=(b == 0), stop=(b == H // PASS - 1))
+            for b in range(H // PASS):
                 codes, plane = h_q[b, j]
                 nc.tensor.matmul_mx(
-                    out=ya[:], lhsT=w8_codes[:, b, cols].bitcast(FP8X4), lhsT_scale=w8_plane[4 * b : P, cols],
-                    rhs=codes[:].bitcast(FP8X4), rhs_scale=plane[:], start=(b == 0), stop=(b == 1))
-            if damp_tag is None:
-                damp = ring3.tile([P, CH], F32, name="damp")
-            else:
-                damp = keep.tile([P, CH], F32, name=damp_tag + "_damp", tag=damp_tag, align_bytes=64)
+                    out=ya[:], lhsT=w8_codes[:, b, cols].bitcast(FP8X4), lhsT_scale=w8_plane[PACK * b : P, cols],
+                    rhs=codes[:].bitcast(FP8X4), rhs_scale=plane[:],
+                    start=(b == 0), stop=(b == H // PASS - 1))
+            return ya, yb
+
+        def damping(yb, damp):
             nc.scalar.activation(out=damp[:], in_=yb[:], func=ACT.Abs)
             nc.scalar.activation(out=damp[:], in_=damp[:], func=ACT.Abs_reciprocal_sqrt, bias=1.0)
             nc.scalar.activation(out=damp[:], in_=damp[:], func=ACT.Square)
-            if on_gpsimd:
-                sums = ring3.tile([P, CH], F32, name="sums")
-                nc.scalar.copy(out=sums[:], in_=ya[:])
-                weight = ring2.tile([P, CH], F32, name="weight")
-                nc.gpsimd.tensor_tensor(out=weight[:], in0=damp[:], in1=factors[:, CH * j : CH * (j + 1)], op=ALU.mult)
-                placed = ring3.tile([P, CH], F32, name="placed")
-                nc.gpsimd.tensor_tensor(out=placed[:], in0=sums[:], in1=weight[:], op=ALU.mult)
-                nc.vector.tensor_copy(pages[c][:].indirect(entries(list3, j)), placed[:])
-                return
+
+        def next_damp():
+            return ring3.tile([P, CHUNK], F32, name="damp")
+
+        def late_slot(shape, dtype, tag, role):
+            return keep.tile(shape, dtype, name=tag + role, tag=tag, align_bytes=64)
+
+        def place_first_chunk(c, make_damp):
+            ya, yb = products(c, 0)
+            damp = make_damp()
+            damping(yb, damp)
             ys = []
-            for u in range(2):
+            for u in range(CHUNK // HALF):
                 y = ring2.tile([P, HALF], F32, name="y%d" % u)
                 nc.vector.tensor_tensor(out=y[:], in0=ya[:, HALF * u : HALF * (u + 1)],
                                         in1=damp[:, HALF * u : HALF * (u + 1)], op=ALU.mult)
                 ys.append(y)
-            for u in range(2):
-                first = CH * j + HALF * u
-                nc.vector.tensor_tensor(out=pages[c][:].indirect(list3[:, first // 16 : (first + HALF) // 16]),
-                                        in0=ys[u][:], in1=factors[:, first : first + HALF], op=ALU.mult)
+            for u in range(CHUNK // HALF):
+                nc.vector.tensor_tensor(out=pages[c][:].indirect(entries(list3, HALF * u, HALF)),
+                                        in0=ys[u][:], in1=factors[:, HALF * u : HALF * (u + 1)], op=ALU.mult)
 
-        second_stage(0, 0, "late0", False)
-        h_rows[1, 1] = stitch_max(1, 1, False)
-        second_stage(1, 0, "late1", False)
-        h_q[0, 1] = quantize(interleave(h_rows[0, 1], nc.scalar.copy, late_tile("late0")), "hq01")
-        h_q[1, 1] = quantize(interleave(h_rows[1, 1], nc.scalar.copy, late_tile("late1")), "hq11")
-        second_stage(2, 0, None, False)
-        second_stage(3, 0, None, False)
+        def place_second_chunk(c):
+            ya, yb = products(c, 1)
+            damp = next_damp()
+            damping(yb, damp)
+            sums = ring3.tile([P, CHUNK], F32, name="sums")
+            nc.scalar.copy(out=sums[:], in_=ya[:])
+            weight = ring2.tile([P, CHUNK], F32, name="weight")
+            nc.gpsimd.tensor_tensor(out=weight[:], in0=damp[:], in1=factors[:, CHUNK:S], op=ALU.mult)
+            placed = ring3.tile([P, CHUNK], F32, name="placed")
+            nc.gpsimd.tensor_tensor(out=placed[:], in0=sums[:], in1=weight[:], op=ALU.mult)
+            nc.vector.tensor_copy(pages[c][:].indirect(entries(list3, CHUNK, CHUNK)), placed[:])
+
+        place_first_chunk(0, lambda: late_slot([P, CHUNK], F32, "late0", "_damp"))
+        h_rows[1, 1] = stitch_max(1, 1, bank_by_bank)
+        place_first_chunk(1, lambda: late_slot([P, CHUNK], F32, "late1", "_damp"))
+        for b in range(H // PASS):
+            grouped = late_slot([P, PASS * PACK], BF16, "late%d" % b, "_late")
+            h_q[b, 1] = quantize(interleave(h_rows[b, 1], nc.scalar.copy, grouped), "hq%d1" % b)
+        place_first_chunk(2, next_damp)
+        place_first_chunk(3, next_damp)
         for c in range(N // P):
-            second_stage(c, 1)
+            place_second_chunk(c)
             nc.sync.dma_start(out=out[P * c : P * (c + 1), :], in_=pages[c][:])

from contextlib import ExitStack

import concourse.mybir as mybir

K, K2, H, N, T, S, T2 = 1024, 512, 1024, 512, 2048, 1024, 2048
FLOPS = 2 * S * (K * H + K2 * H + 2 * H * N)

F32 = mybir.dt.float32
BF16 = mybir.dt.bfloat16
I32 = mybir.dt.int32
U32 = mybir.dt.uint32
U16 = mybir.dt.uint16
U8 = mybir.dt.uint8
FP8X4 = mybir.dt.float8_e4m3fn_x4
FP4X4 = mybir.dt.float4_e2m1fn_x4
ACT = mybir.ActivationFunctionType
ALU = mybir.AluOpType

P = 128
PACK = 4
PASS = P * PACK
QUADRANT = 32
QUADRANTS = P // QUADRANT
GROUP = 16
CHUNK = 512
CHUNKS = S // CHUNK
HALF = CHUNK // 2
LINE = 4
SCALAR_BANKS = 3
VECTOR_BANKS = 5


def tile_list_stitch_pull_features_kernel(
    tc, tab_words, tab_scales, offs, tab2_words, tab2_scales, offs2, offs3,
    w1, w4_words, w4_scales, gain, w8_words, w8_scales, wb, wgo, page1, out,
):
    nc = tc.nc
    with ExitStack() as ctx:
        keep = ctx.enter_context(tc.tile_pool(name="keep", bufs=1))
        ring2 = ctx.enter_context(tc.tile_pool(name="ring2", bufs=2))
        ring3 = ctx.enter_context(tc.tile_pool(name="ring3", bufs=3))
        ps_s = ctx.enter_context(tc.psum_pool(name="ps_s", bufs=SCALAR_BANKS))
        ps_v = ctx.enter_context(tc.psum_pool(name="ps_v", bufs=VECTOR_BANKS))

        def load_list(src, name):
            offsets = keep.tile([P, S // GROUP], U16, name=name)
            nc.sync.dma_start(offsets[:], src)
            return offsets

        def entries(offsets, first, count):
            return offsets[:, first // GROUP : (first + count) // GROUP]

        def load_plane(dst, rows):
            for d in range(QUADRANTS):
                nc.sync.dma_start(
                    out=dst[QUADRANT * d : QUADRANT * (d + 1), :].bitcast(I32),
                    in_=rows[PACK * d : PACK * (d + 1), :].bitcast(I32).partition_broadcast(QUADRANT // PACK))

        def load_rows(src, tag):
            raw = keep.tile([P, PACK, PASS], F32, name=tag + "_raw", tag=tag, align_bytes=64)
            nc.sync.dma_start(out=raw[:], in_=src.rearrange("(p j) c -> p j c", j=PACK))
            return raw

        def load_table(src, tag):
            window = keep.tile([P, T], U32, name=tag + "_win", tag=tag, align_bytes=64)
            nc.sync.dma_start(out=window[:].bitcast(I32), in_=src.rearrange("p t i -> p (t i)").bitcast(I32))
            return window

        def gather_words(window, offsets, name):
            picked = []
            for j in range(CHUNKS):
                codes = keep.tile([P, CHUNK], U32, name="%s_%d" % (name, j), align_bytes=64)
                nc.vector.tensor_copy(codes[:], window[:].indirect(entries(offsets, CHUNK * j, CHUNK)))
                picked.append(codes)
            return picked

        def next_grouped():
            return ring3.tile([P, PASS * PACK], BF16, name="grouped", align_bytes=64)

        def interleave(rows, copy, grouped):
            copy(out=grouped[:].rearrange("p (c i t) -> p c t i", i=LINE, t=PACK),
                 in_=rows[:].rearrange("p t (c i) -> p c t i", i=LINE))
            return grouped[:]

        def deal_and_interleave(raw):
            grouped = next_grouped()
            nc.scalar.copy(out=grouped[:].rearrange("p (t m j) -> p m j t", t=PACK, j=PACK),
                           in_=raw[:].rearrange("p j (m t) -> p m j t", t=PACK))
            return grouped[:]

        def quantize(grouped, name):
            codes = keep.tile([P, PASS], U32, name=name + "_codes", align_bytes=64)
            plane = keep.tile([P, PASS], U8, name=name + "_plane", align_bytes=64)
            nc.vector.quantize_mx(out=codes[:].bitcast(FP8X4), scales=plane[:], in_=grouped)
            return codes, plane

        v2s_win = keep.tile([P, T], U8, name="v2s_win", align_bytes=64)
        vs_win = keep.tile([P, T], U8, name="vs_win", align_bytes=64)
        w4s_raw = keep.tile([P, H], U8, name="w4s_raw", align_bytes=64)
        w8_plane = keep.tile([P, N], U8, name="w8_plane", align_bytes=64)
        nc.gpsimd.memset(vs_win[:].bitcast(I32), 0)
        nc.gpsimd.memset(w8_plane[:].bitcast(I32), 0)

        list2 = load_list(offs2, "list2")
        load_plane(v2s_win, tab2_scales[0])
        list1 = load_list(offs, "list1")
        nc.sync.dma_start(out=vs_win[0:P:PACK, :].bitcast(I32),
                          in_=tab_scales.rearrange("a q t -> q a t").bitcast(I32))
        w1_raw = {}
        w1_raw[0, 0] = load_rows(w1[0:PASS, 0:PASS], "slot0")
        w4_raw = keep.tile([P, 2 * H], U8, name="w4_raw", align_bytes=64)
        nc.sync.dma_start(out=w4_raw[:].bitcast(I32), in_=w4_words[0].bitcast(I32))
        v2_win = load_table(tab2_words[0], "v2_win")
        load_plane(w4s_raw, w4_scales[0])
        w1_raw[1, 0] = load_rows(w1[PASS:K, 0:PASS], "slot1")
        gains = keep.tile([P, H // PASS, PACK], F32, name="gains")
        nc.gpsimd.dma_start(out=gains[:], in_=gain.rearrange("(b p t) -> p b t", p=P, t=PACK))
        v_win = [load_table(tab_words[0], "v_win0")]

        v2_plane = keep.tile([P, S], U8, name="v2_plane", align_bytes=64)
        nc.vector.tensor_copy(v2_plane[:], v2s_win[:].indirect(list2[:]))
        first_grouped = deal_and_interleave(w1_raw[0, 0])
        vs_picked = keep.tile([P, S], U8, name="vs_picked", align_bytes=64)
        nc.vector.tensor_copy(vs_picked[:], vs_win[:].indirect(list1[:]))
        v_plane = keep.tile([P, S], U8, name="v_plane", align_bytes=64)
        nc.vector.tensor_copy(v_plane[:].bitcast(I32), vs_picked[:].bitcast(I32))
        span = QUADRANT * (QUADRANTS - 1) + PACK + 1
        for r in range(1, PACK):
            nc.sync.dma_start(out=v_plane[r : r + span : PACK, :].bitcast(I32),
                              in_=vs_picked[8 * r : 8 * r + span : PACK, :].bitcast(I32))

        w1_raw[0, 1] = load_rows(w1[0:PASS, PASS:H], "slot2")
        v_win.append(load_table(tab_words[1], "v_win1"))
        w1_raw[1, 1] = load_rows(w1[PASS:K, PASS:H], "slot3")
        wb_raw = [load_rows(wb[PASS * b : PASS * (b + 1), :], "wb%d" % b) for b in range(H // PASS)]
        w8_codes = keep.tile([P, H // PASS, N], U32, name="w8_codes", align_bytes=64)
        nc.sync.dma_start(out=w8_codes[:].bitcast(I32),
                          in_=w8_words.rearrange("a p c i -> p a (c i)").bitcast(I32))
        for d in range(QUADRANTS):
            nc.gpsimd.dma_start(out=w8_plane[QUADRANT * d : QUADRANT * d + 2 * PACK, :].bitcast(I32),
                                in_=w8_scales[:, PACK * d : PACK * (d + 1), :].bitcast(I32))
        factors = keep.tile([P, S], F32, name="factors")
        nc.sync.dma_start(out=factors[:], in_=wgo)
        list3 = load_list(offs3, "list3")
        pages = []
        for c in range(N // P):
            page = keep.tile([P, T2], F32, name="page%d" % c)
            nc.sync.dma_start(out=page[:], in_=page1[P * c : P * (c + 1), :])
            pages.append(page)

        w4_dealt = keep.tile([P, 2 * H], U8, name="w4_dealt", align_bytes=64)
        nc.vector.tensor_copy(
            out=w4_dealt[:].bitcast(U16).rearrange("p (b t m) -> p b t m", b=H // PASS, t=PACK),
            in_=w4_raw[:].bitcast(U16).rearrange("p (b m t) -> p b t m", b=H // PASS, t=PACK))
        v2_codes = gather_words(v2_win, list2, "v2_codes")
        w4_plane = keep.tile([P, H], U8, name="w4_plane", align_bytes=64)
        nc.vector.tensor_copy(
            out=w4_plane[:].rearrange("p (b t m) -> p b t m", b=H // PASS, t=PACK),
            in_=w4s_raw[:].rearrange("p (b m t) -> p b t m", b=H // PASS, t=PACK))

        def fabric_tanh(b, j, tag):
            tanh = keep.tile([P, PACK, CHUNK], F32, name=tag + "_tanh", tag=tag, align_bytes=64)
            for t in range(PACK):
                col = PASS * b + P * t
                acc = ps_s.tile([P, CHUNK], F32, name="acc_s")
                nc.tensor.matmul_mx(
                    out=acc[:],
                    lhsT=w4_dealt[:, 2 * col : 2 * (col + P)].bitcast(FP4X4),
                    lhsT_scale=w4_plane[:, col : col + P],
                    rhs=v2_codes[j][:].bitcast(FP8X4),
                    rhs_scale=v2_plane[:, CHUNK * j : CHUNK * (j + 1)],
                    start=True, stop=True)
                nc.scalar.activation(out=tanh[:, t, :], in_=acc[:], func=ACT.Tanh)
            return tanh

        w1_q = {}
        tanhs = {}
        w1_q[0, 0] = quantize(first_grouped, "w1q00")
        w1_q[1, 0] = quantize(deal_and_interleave(w1_raw[1, 0]), "w1q10")
        tanhs[0, 0] = fabric_tanh(0, 0, "slot1")
        v_codes = [gather_words(v_win[0], list1, "v_codes0")]
        w1_q[0, 1] = quantize(deal_and_interleave(w1_raw[0, 1]), "w1q01")
        tanhs[1, 0] = fabric_tanh(1, 0, "slot2")
        v_codes.append(gather_words(v_win[1], list1, "v_codes1"))
        w1_q[1, 1] = quantize(deal_and_interleave(w1_raw[1, 1]), "w1q11")

        pass_by_pass = [(a, t) for a in range(K // PASS) for t in range(PACK)]
        bank_by_bank = [(a, t) for t in range(PACK) for a in range(K // PASS)]

        def stitch_max(b, j, order):
            rows = keep.tile([P, PACK, CHUNK], BF16, name="h_rows%d%d" % (b, j), align_bytes=64)
            accs = [ps_v.tile([P, CHUNK], F32, name="acc_v") for t in range(PACK)]
            for a, t in order:
                codes, plane = w1_q[a, b]
                nc.tensor.matmul_mx(
                    out=accs[t][:],
                    lhsT=codes[:, P * t : P * (t + 1)].bitcast(FP8X4),
                    lhsT_scale=plane[:, P * t : P * (t + 1)],
                    rhs=v_codes[a][j][:].bitcast(FP8X4),
                    rhs_scale=v_plane[PACK * a : P, CHUNK * j : CHUNK * (j + 1)],
                    start=(a == 0), stop=(a == K // PASS - 1))
            for t in range(PACK):
                nc.vector.scalar_tensor_tensor(
                    out=rows[:, t, :], in0=tanhs[b, j][:, t, :], scalar=gains[:, b, t : t + 1],
                    in1=accs[t][:], op0=ALU.mult, op1=ALU.max)
            return rows

        h_q = {}
        h_rows = {}
        h_rows[0, 0] = stitch_max(0, 0, pass_by_pass)
        h_rows[1, 0] = stitch_max(1, 0, pass_by_pass)
        h_grouped = interleave(h_rows[0, 0], nc.scalar.copy, next_grouped())
        wb_q = [quantize(interleave(wb_raw[b], nc.vector.tensor_copy, next_grouped()), "wbq%d" % b)
                for b in range(H // PASS)]
        h_q[0, 0] = quantize(h_grouped, "hq00")
        h_q[1, 0] = quantize(interleave(h_rows[1, 0], nc.scalar.copy, next_grouped()), "hq10")
        tanhs[0, 1] = fabric_tanh(0, 1, "slot3")
        tanhs[1, 1] = fabric_tanh(1, 1, "slot0")
        preload = keep.tile([P, 1], F32, name="preload")
        nc.scalar.activation(out=preload[:], in_=tanhs[1, 1][:, PACK - 1, CHUNK - 1 : CHUNK],
                             func=ACT.Abs_reciprocal_sqrt, bias=2.0)
        h_rows[0, 1] = stitch_max(0, 1, bank_by_bank)

        def products(c, j):
            cols = slice(P * c, P * (c + 1))
            yb = ps_s.tile([P, CHUNK], F32, name="acc_s")
            ya = ps_v.tile([P, CHUNK], F32, name="acc_v")
            for b in range(H // PASS):
                codes, plane = h_q[b, j]
                nc.tensor.matmul_mx(
                    out=yb[:], lhsT=wb_q[b][0][:, cols].bitcast(FP8X4), lhsT_scale=wb_q[b][1][:, cols],
                    rhs=codes[:].bitcast(FP8X4), rhs_scale=plane[:],
                    start=(b == 0), stop=(b == H // PASS - 1))
            for b in range(H // PASS):
                codes, plane = h_q[b, j]
                nc.tensor.matmul_mx(
                    out=ya[:], lhsT=w8_codes[:, b, cols].bitcast(FP8X4), lhsT_scale=w8_plane[PACK * b : P, cols],
                    rhs=codes[:].bitcast(FP8X4), rhs_scale=plane[:],
                    start=(b == 0), stop=(b == H // PASS - 1))
            return ya, yb

        def damping(yb, damp):
            nc.scalar.activation(out=damp[:], in_=yb[:], func=ACT.Abs)
            nc.scalar.activation(out=damp[:], in_=damp[:], func=ACT.Abs_reciprocal_sqrt, bias=1.0)
            nc.scalar.activation(out=damp[:], in_=damp[:], func=ACT.Square)

        def next_damp():
            return ring3.tile([P, CHUNK], F32, name="damp")

        def late_slot(shape, dtype, tag, role):
            return keep.tile(shape, dtype, name=tag + role, tag=tag, align_bytes=64)

        def place_first_chunk(c, make_damp):
            ya, yb = products(c, 0)
            damp = make_damp()
            damping(yb, damp)
            ys = []
            for u in range(CHUNK // HALF):
                y = ring2.tile([P, HALF], F32, name="y%d" % u)
                nc.vector.tensor_tensor(out=y[:], in0=ya[:, HALF * u : HALF * (u + 1)],
                                        in1=damp[:, HALF * u : HALF * (u + 1)], op=ALU.mult)
                ys.append(y)
            for u in range(CHUNK // HALF):
                nc.vector.tensor_tensor(out=pages[c][:].indirect(entries(list3, HALF * u, HALF)),
                                        in0=ys[u][:], in1=factors[:, HALF * u : HALF * (u + 1)], op=ALU.mult)

        def place_second_chunk(c):
            ya, yb = products(c, 1)
            damp = next_damp()
            damping(yb, damp)
            sums = ring3.tile([P, CHUNK], F32, name="sums")
            nc.scalar.copy(out=sums[:], in_=ya[:])
            weight = ring2.tile([P, CHUNK], F32, name="weight")
            nc.gpsimd.tensor_tensor(out=weight[:], in0=damp[:], in1=factors[:, CHUNK:S], op=ALU.mult)
            placed = ring3.tile([P, CHUNK], F32, name="placed")
            nc.gpsimd.tensor_tensor(out=placed[:], in0=sums[:], in1=weight[:], op=ALU.mult)
            nc.vector.tensor_copy(pages[c][:].indirect(entries(list3, CHUNK, CHUNK)), placed[:])

        place_first_chunk(0, lambda: late_slot([P, CHUNK], F32, "late0", "_damp"))
        h_rows[1, 1] = stitch_max(1, 1, bank_by_bank)
        place_first_chunk(1, lambda: late_slot([P, CHUNK], F32, "late1", "_damp"))
        for b in range(H // PASS):
            grouped = late_slot([P, PASS * PACK], BF16, "late%d" % b, "_late")
            h_q[b, 1] = quantize(interleave(h_rows[b, 1], nc.scalar.copy, grouped), "hq%d1" % b)
        place_first_chunk(2, next_damp)
        place_first_chunk(3, next_damp)
        for c in range(N // P):
            place_second_chunk(c)
            nc.sync.dma_start(out=out[P * c : P * (c + 1), :], in_=pages[c][:])
